import numpy as np
import ml_dtypes


def mxq(x, axis, fmt="e4m3"):
    dtype, down = {"e4m3": (ml_dtypes.float8_e4m3fn, 7), "e5m2": (ml_dtypes.float8_e5m2, 14)}[fmt]
    v = np.moveaxis(np.asarray(x, np.float32).astype(ml_dtypes.bfloat16).astype(np.float64), axis, -1)
    blocks = v.reshape(v.shape[:-1] + (-1, 32))
    amax = np.abs(blocks).max(-1, keepdims=True)
    byte = np.maximum(np.where(amax > 0, np.frexp(amax)[1] - 1 + 127, 0) - down, 1)
    scale = np.exp2(byte - 127.0)
    codes = (blocks / scale).astype(np.float32).astype(dtype).astype(np.float64)
    return np.moveaxis((codes * scale).reshape(v.shape), -1, axis)


WIDE = False


def mx_kscale(k):
    if not WIDE:
        return np.ones(k)
    levels = np.array([10, -10, 5, -5, 0])
    if k % 512:
        return np.exp2(np.random.permutation(np.resize(levels, k // 32))).repeat(32)
    a = np.empty((k // 512, 16))
    for p in range(k // 512):
        a[p, :8] = np.random.permutation(np.resize(levels, 8))
        for g in range(8):
            far = levels[np.abs(levels - a[p, g]) >= 10]
            a[p, g + 8] = far[np.random.randint(len(far))]
    return np.exp2(a.ravel()).repeat(32)


def f64(x):
    return np.asarray(x).astype(np.float64)


def striped(idx):
    return np.tile(idx.reshape(-1, 16).T, (8, 1)).astype(np.uint16)


def unstriped(offs):
    return offs[:16].T.reshape(-1).astype(np.int64)


def striped8(idx):
    return np.concatenate([x.reshape(-1, 16).T for x in idx]).astype(np.uint16)


def runs(offs, k):
    lists = np.stack([offs[16 * r : 16 * r + 16].T.reshape(-1) for r in range(8)]).astype(np.int64)
    return lists[np.arange(k) % 512 // 64]


def pack_weight(w):
    k, n = w.shape
    w = f64(np.asarray(w, np.float32).astype(ml_dtypes.bfloat16)).reshape(k // 32, 32, n)
    amax = np.abs(w).max(1)
    byte = np.clip(np.where(amax > 0, np.frexp(amax)[1] - 1 + 127 - 7, 1), 1, 254)
    scaled = (w * np.exp2(127.0 - byte)[:, None, :]).reshape(k, n).astype(np.float32)
    words = np.ascontiguousarray(scaled.reshape(k // 512, 128, 4, n).transpose(0, 1, 3, 2)).astype(ml_dtypes.float8_e4m3fn).view(np.uint8)
    return words, np.ascontiguousarray(byte.astype(np.uint8).reshape(k // 512, 16, n))


def unpack_weight(words, scales):
    g, p, n, _ = words.shape
    vals = np.ascontiguousarray(words).view(ml_dtypes.float8_e4m3fn).astype(np.float64) * np.repeat(np.exp2(scales.astype(np.float64) - 127.0), 8, axis=1)[..., None]
    return vals.transpose(0, 1, 3, 2).reshape(g * 512, n)


K, T, S, V, H, U = 512, 2048, 512, 512, 512, 1024


def setup_inputs():
    n = np.random.standard_normal
    s = mx_kscale(K)[:, None]
    u = mx_kscale(S)
    packed_xT = pack_weight(n((K, T)) * s)
    return {
        "x_words": packed_xT[0],
        "x_scales": packed_xT[1],
        "w1": (n((K, H)) / np.sqrt(K) / s).astype(np.float32),
        "w2": (n((K, H)) / np.sqrt(K) / s).astype(np.float32),
        "mem": n((H, U)).astype(np.float32),
        "ga": (np.random.uniform(0.5, 1.5, (H, 1)) * u[:, None]).astype(np.float32),
        "gb": (np.random.uniform(0.5, 1.5, (H, 1)) / u[:, None]).astype(np.float32),
        "offs": striped(np.random.permutation(T)[:S]),
        "two": striped(np.random.permutation(T)[:V]),
        "slot": striped8(np.stack([np.random.permutation(U)[:S] for _ in range(8)])),
        "nq": striped8(np.stack([np.random.permutation(V) for _ in range(8)])),
    }


def reference(x_words, x_scales, w1, w2, mem, ga, gb, offs, two, slot, nq):
    xq = unpack_weight(x_words, x_scales)[:, unstriped(offs)]
    a = mxq(f64(w1), 0, "e4m3").T @ xq
    pg = f64(mem).copy()
    pg[np.arange(H)[:, None], runs(slot, H)] = a
    z = f64(ga) * pg
    x_two = unpack_weight(x_words, x_scales)[:, unstriped(two)]
    b = mxq(f64(w2), 0, "e4m3").T @ x_two
    z2 = f64(gb) * (np.maximum(b, b[np.arange(H)[:, None], runs(nq, H)]))
    s = 0.0625 * ((mxq(z, 0, "e4m3").T @ mxq(z2, 0, "e4m3")))
    return np.tanh(s)

@@ -1,0 +1,236 @@
+from contextlib import ExitStack
+
+import concourse.mybir as mybir
+
+F32 = mybir.dt.float32
+BF16 = mybir.dt.bfloat16
+I32 = mybir.dt.int32
+U32 = mybir.dt.uint32
+U16 = mybir.dt.uint16
+U8 = mybir.dt.uint8
+FP8X4 = mybir.dt.float8_e4m3fn_x4
+ALU = mybir.AluOpType
+ACT = mybir.ActivationFunctionType
+
+K, T, S, V, H, U = 512, 2048, 512, 512, 512, 1024
+P = 128
+PACK = 4
+BANK = 512
+PER_COLUMN = 16
+FLOPS = 2 * K * H * S + 2 * K * H * V + 2 * H * U * V
+
+W1_VECTOR_M = 80
+SLOT_CHUNK = 512
+QUERY_CHUNKS = (256, 128, 128)
+
+
+def tile_picked_keypage_none_p_kernel(
+    tc, x_words, x_scales, w1, w2, mem, ga, gb, offs, two, slot, nq, out
+):
+    nc = tc.nc
+    with ExitStack() as ctx:
+        lists = ctx.enter_context(tc.tile_pool(name="lists", bufs=1))
+        keep = ctx.enter_context(tc.tile_pool(name="keep", bufs=1))
+        psum = ctx.enter_context(tc.psum_pool(name="psum", bufs=1))
+
+        def sb(name, shape, dtype, reuse=None):
+            return keep.tile(shape, dtype, name=name, tag=reuse or name, align_bytes=64)
+
+        def bank(i):
+            return psum.tile([P, BANK], F32, name=f"bank{i}", tag=f"bank{i}")
+
+        def load_list(name, source):
+            tile = lists.tile([P, S // PER_COLUMN], U16, name=name)
+            nc.sync.dma_start(tile[:], source)
+            return tile
+
+        def load_weight(name, w):
+            raw = sb(name, [P, PACK, H], F32)
+            nc.sync.dma_start(raw[:], w.rearrange("(p j) c -> p j c", j=PACK))
+            return raw
+
+        def load_feature_weights(name, g):
+            tile = sb(name, [P, PACK], F32)
+            nc.sync.dma_start(tile[:], g.rearrange("(p t) o -> p (t o)", t=PACK))
+            return tile
+
+        def load_page(t):
+            tile = sb(f"page{t}", [P, U], F32)
+            nc.sync.dma_start(tile[:], mem.rearrange("(p t) w -> p t w", t=PACK)[:, t, :])
+            return tile
+
+        def quantize(name, grouped, width):
+            codes = sb(f"{name}_codes", [P, width], U32)
+            scales = sb(f"{name}_scales", [P, width], U8)
+            nc.vector.quantize_mx(out=codes[:].bitcast(FP8X4), scales=scales[:], in_=grouped)
+            return codes, scales
+
+        def product(acc, stationary, columns, moving):
+            nc.tensor.matmul_mx(
+                out=acc,
+                lhsT=stationary[0][:, columns].bitcast(FP8X4),
+                lhsT_scale=stationary[1][:, columns],
+                rhs=moving[0][:].bitcast(FP8X4),
+                rhs_scale=moving[1][:],
+                start=True,
+                stop=True,
+            )
+
+        w1_raw = sb("w1_raw", [P, PACK, H], F32)
+        w1_rows = w1.rearrange("(p j) c -> p j c", j=PACK)
+        nc.sync.dma_start(w1_raw[:, :1, :], w1_rows[:, :1, :])
+        offs_list = load_list("offs_list", offs)
+        two_list = load_list("two_list", two)
+        x_scale_table = sb("x_scale_table", [P, T], U8)
+        nc.vector.memset(x_scale_table[:].bitcast(I32), 0)
+        for q in range(4):
+            nc.sync.dma_start(
+                x_scale_table[32 * q : 32 * q + 4, :].bitcast(I32),
+                x_scales[0, 4 * q : 4 * q + 4, :].bitcast(I32),
+            )
+        warm = sb("warm", [P, 1], F32)
+        warm_out = sb("warm_out", [P, 1], F32)
+        nc.gpsimd.memset(warm[:], 0.0)
+        nc.scalar.activation(warm_out[:], warm[:], ACT.Tanh)
+
+        nc.sync.dma_start(w1_raw[:, 1:, :], w1_rows[:, 1:, :])
+        x_word_table = sb("x_word_table", [P, T], U32)
+        nc.sync.dma_start(
+            x_word_table[:].bitcast(I32),
+            x_words[0].rearrange("p n r -> p (n r)").bitcast(I32),
+        )
+        ga_raw = load_feature_weights("ga_raw", ga)
+        gb_raw = load_feature_weights("gb_raw", gb)
+        slot_list = load_list("slot_list", slot)
+        pages = [load_page(0)]
+        w2_raw = load_weight("w2_raw", w2)
+        pages.append(load_page(1))
+        nq_list = load_list("nq_list", nq)
+        pages.append(load_page(2))
+        pages.append(load_page(3))
+
+        def gather(name, table, offsets, dtype):
+            picked = sb(name, [P, S], dtype)
+            nc.vector.tensor_copy(picked[:], table[:].indirect(offsets[:]))
+            return picked
+
+        xa_scales = gather("xa_scales", x_scale_table, offs_list, U8)
+        xb_scales = gather("xb_scales", x_scale_table, two_list, U8)
+
+        def cast_views(raw, grouped):
+            return (
+                grouped[:].rearrange("p (t m j) -> p m j t", t=PACK, j=PACK),
+                raw[:].rearrange("p j (m t) -> p m j t", t=PACK),
+            )
+
+        w1_grouped = sb("w1_grouped", [P, PACK * H], BF16)
+        dst, src = cast_views(w1_raw, w1_grouped)
+        nc.vector.tensor_copy(dst[:, :W1_VECTOR_M], src[:, :W1_VECTOR_M])
+        nc.scalar.copy(dst[:, W1_VECTOR_M:], src[:, W1_VECTOR_M:])
+
+        twice_nonneg = sb("twice_nonneg", [P, PACK], F32)
+        ga_signed = sb("ga_signed", [P, PACK], F32)
+        gb_abs = sb("gb_abs", [P, PACK], F32)
+        nc.vector.tensor_scalar(twice_nonneg[:], gb_raw[:], 0.0, 2.0, ALU.is_ge, ALU.mult)
+        w1_q = quantize("w1", w1_grouped[:], H)
+        nc.vector.scalar_tensor_tensor(ga_signed[:], twice_nonneg[:], -1.0, ga_raw[:], ALU.add, ALU.mult)
+        nc.vector.scalar_tensor_tensor(gb_abs[:], twice_nonneg[:], -1.0, gb_raw[:], ALU.add, ALU.mult)
+
+        xa = (gather("xa_words", x_word_table, offs_list, U32), xa_scales)
+        a_rows = []
+        for t in range(PACK):
+            acc = bank(t)
+            product(acc[:], w1_q, slice(P * t, P * (t + 1)), xa)
+            a_t = sb(f"a{t}", [P, S], F32)
+            nc.scalar.copy(a_t[:], acc[:])
+            a_rows.append(a_t)
+        xb = (gather("xb_words", x_word_table, two_list, U32), xb_scales)
+
+        slot_chunks = U // SLOT_CHUNK
+        z_pairs = []
+        z_grouped = []
+
+        def write_page(t):
+            nc.vector.tensor_copy(pages[t][:].indirect(slot_list[:]), a_rows[t][:])
+
+        def scale_page(t, c):
+            nc.scalar.activation(
+                z_pairs[c][:, t // 2, :, t % 2],
+                pages[t][:, c * SLOT_CHUNK : (c + 1) * SLOT_CHUNK],
+                ACT.Copy,
+                scale=ga_signed[:, t : t + 1],
+            )
+
+        def group_page(c):
+            grouped = sb(f"z_grouped{c}", [P, SLOT_CHUNK * PACK], BF16)
+            nc.scalar.copy(
+                grouped[:].bitcast(F32).rearrange("p (c i u) -> p c u i", i=4, u=2),
+                z_pairs[c][:].rearrange("p u w e -> p u (w e)").bitcast(F32).rearrange("p u (c i) -> p c u i", i=4),
+            )
+            return grouped
+
+        write_page(0)
+        w2_grouped = sb("w2_grouped", [P, PACK * H], BF16)
+        dst, src = cast_views(w2_raw, w2_grouped)
+        nc.scalar.copy(dst, src)
+        write_page(1)
+        w2_q = quantize("w2", w2_grouped[:], H)
+        z_pairs.append(sb("z_pairs0", [P, 2, SLOT_CHUNK, 2], BF16, reuse="w2_raw"))
+        z_pairs.append(sb("z_pairs1", [P, 2, SLOT_CHUNK, 2], BF16, reuse="w2_grouped"))
+        scale_page(0, 0)
+        b_rows = []
+        b_all = sb("b_all", [P, PACK, V], F32)
+        for t in range(PACK):
+            acc = bank(PACK + t)
+            product(acc[:], w2_q, slice(P * t, P * (t + 1)), xb)
+            b_t = sb(f"b{t}", [P, V], F32)
+            nc.scalar.activation(b_t[:], acc[:], ACT.Copy, scale=gb_abs[:, t : t + 1])
+            nc.sync.dma_start(b_all[:, t, :], b_t[:])
+            b_rows.append(b_t)
+        scale_page(0, 1)
+        for t in range(1, PACK):
+            if t > 1:
+                write_page(t)
+            for c in range(slot_chunks):
+                scale_page(t, c)
+                if t == PACK - 1:
+                    z_grouped.append(group_page(c))
+
+        def neighbours(n, v0, width):
+            reuse = ("a3", "z_grouped1", None)[n]
+            fetched = sb(f"fetched{n}", [P, PACK, width], F32, reuse=reuse)
+            columns = slice(v0 // PER_COLUMN, (v0 + width) // PER_COLUMN)
+            for t in range(PACK):
+                nc.vector.tensor_copy(fetched[:, t, :], b_rows[t][:].indirect(nq_list[:, columns]))
+            grouped = sb(f"z2_grouped{n}", [P, width * PACK], BF16)
+            nc.vector.tensor_tensor(
+                grouped[:].rearrange("p (c i t) -> p c t i", i=4, t=PACK),
+                b_all[:, :, v0 : v0 + width].rearrange("p t (c i) -> p c t i", i=4),
+                fetched[:].rearrange("p t (c i) -> p c t i", i=4),
+                ALU.max,
+            )
+            return grouped
+
+        out_rows = out.rearrange("(b p) v -> p b v", p=P)
+        blocks_per_chunk = SLOT_CHUNK // P
+        z_q = []
+        next_bank = 0
+        v0 = 0
+        for n, width in enumerate(QUERY_CHUNKS):
+            z2_grouped = neighbours(n, v0, width)
+            if n == 0:
+                z_q.append(quantize("z0", z_grouped[0][:], SLOT_CHUNK))
+            z2_q = quantize(f"z2_{n}", z2_grouped[:], width)
+            if n == 0:
+                z_q.append(quantize("z1", z_grouped[1][:], SLOT_CHUNK))
+            per_bank = BANK // width
+            for first in range(0, U // P, per_bank):
+                acc = bank(next_bank)
+                for g in range(per_bank):
+                    c, block = divmod(first + g, blocks_per_chunk)
+                    product(acc[:, g * width : (g + 1) * width], z_q[c], slice(P * block, P * (block + 1)), z2_q)
+                scores = sb(f"scores{next_bank}", [P, per_bank, width], F32)
+                nc.scalar.activation(scores[:].rearrange("p g v -> p (g v)"), acc[:], ACT.Tanh, scale=0.0625)
+                nc.sync.dma_start(out_rows[:, first : first + per_bank, v0 : v0 + width], scores[:])
+                next_bank = next_bank + 1
+            v0 = v0 + width

@@ -19,7 +19,7 @@ BANK = 512
 PER_COLUMN = 16
 FLOPS = 2 * K * H * S + 2 * K * H * V + 2 * H * U * V
 
-W1_VECTOR_M = 80
+W1_VECTOR_M = 24
 SLOT_CHUNK = 512
 QUERY_CHUNKS = (256, 128, 128)
 
@@ -76,9 +76,9 @@ def tile_picked_keypage_none_p_kernel(
                 stop=True,
             )
 
-        w1_raw = sb("w1_raw", [P, PACK, H], F32)
-        w1_rows = w1.rearrange("(p j) c -> p j c", j=PACK)
-        nc.sync.dma_start(w1_raw[:, :1, :], w1_rows[:, :1, :])
+        x_word_table = sb("x_word_table", [P, T], U32)
+        x_word_rows = x_words[0].rearrange("p n r -> p (n r)").bitcast(I32)
+        nc.sync.dma_start(x_word_table[:, : T // 2].bitcast(I32), x_word_rows[:, : T // 2])
         offs_list = load_list("offs_list", offs)
         two_list = load_list("two_list", two)
         x_scale_table = sb("x_scale_table", [P, T], U8)
@@ -93,24 +93,20 @@ def tile_picked_keypage_none_p_kernel(
         nc.gpsimd.memset(warm[:], 0.0)
         nc.scalar.activation(warm_out[:], warm[:], ACT.Tanh)
 
-        nc.sync.dma_start(w1_raw[:, 1:, :], w1_rows[:, 1:, :])
-        x_word_table = sb("x_word_table", [P, T], U32)
-        nc.sync.dma_start(
-            x_word_table[:].bitcast(I32),
-            x_words[0].rearrange("p n r -> p (n r)").bitcast(I32),
-        )
+        w1_raw = load_weight("w1_raw", w1)
+        nc.sync.dma_start(x_word_table[:, T // 2 :].bitcast(I32), x_word_rows[:, T // 2 :])
         ga_raw = load_feature_weights("ga_raw", ga)
         gb_raw = load_feature_weights("gb_raw", gb)
         slot_list = load_list("slot_list", slot)
         pages = [load_page(0)]
         w2_raw = load_weight("w2_raw", w2)
         pages.append(load_page(1))
-        nq_list = load_list("nq_list", nq)
         pages.append(load_page(2))
         pages.append(load_page(3))
+        nq_list = load_list("nq_list", nq)
 
-        def gather(name, table, offsets, dtype):
-            picked = sb(name, [P, S], dtype)
+        def gather(name, table, offsets, dtype, reuse=None):
+            picked = sb(name, [P, S], dtype, reuse=reuse)
             nc.vector.tensor_copy(picked[:], table[:].indirect(offsets[:]))
             return picked
 
@@ -128,34 +124,34 @@ def tile_picked_keypage_none_p_kernel(
         nc.vector.tensor_copy(dst[:, :W1_VECTOR_M], src[:, :W1_VECTOR_M])
         nc.scalar.copy(dst[:, W1_VECTOR_M:], src[:, W1_VECTOR_M:])
 
+        xa = (gather("xa_words", x_word_table, offs_list, U32), xa_scales)
+        half = PACK * H // 2
+        w1_q = [quantize(f"w1_{u}", w1_grouped[:, u * half : (u + 1) * half], H // 2) for u in range(2)]
+        a_all = sb("a_all", [P, PACK * S], F32)
+        a_rows = [a_all[:, S * t : S * (t + 1)] for t in range(PACK)]
+        for t in range(PACK):
+            acc = bank(t)
+            product(acc[:], w1_q[t // 2], slice(P * (t % 2), P * (t % 2 + 1)), xa)
+            nc.scalar.copy(a_rows[t], acc[:])
+        xb = (gather("xb_words", x_word_table, two_list, U32, reuse="w1_raw"), xb_scales)
+
         twice_nonneg = sb("twice_nonneg", [P, PACK], F32)
         ga_signed = sb("ga_signed", [P, PACK], F32)
         gb_abs = sb("gb_abs", [P, PACK], F32)
         nc.vector.tensor_scalar(twice_nonneg[:], gb_raw[:], 0.0, 2.0, ALU.is_ge, ALU.mult)
-        w1_q = quantize("w1", w1_grouped[:], H)
         nc.vector.scalar_tensor_tensor(ga_signed[:], twice_nonneg[:], -1.0, ga_raw[:], ALU.add, ALU.mult)
         nc.vector.scalar_tensor_tensor(gb_abs[:], twice_nonneg[:], -1.0, gb_raw[:], ALU.add, ALU.mult)
-
-        xa = (gather("xa_words", x_word_table, offs_list, U32), xa_scales)
-        a_rows = []
-        for t in range(PACK):
-            acc = bank(t)
-            product(acc[:], w1_q, slice(P * t, P * (t + 1)), xa)
-            a_t = sb(f"a{t}", [P, S], F32)
-            nc.scalar.copy(a_t[:], acc[:])
-            a_rows.append(a_t)
-        xb = (gather("xb_words", x_word_table, two_list, U32), xb_scales)
 
         slot_chunks = U // SLOT_CHUNK
         z_pairs = []
         z_grouped = []
 
         def write_page(t):
-            nc.vector.tensor_copy(pages[t][:].indirect(slot_list[:]), a_rows[t][:])
+            nc.vector.tensor_copy(pages[t][:].indirect(slot_list[:]), a_rows[t])
 
         def scale_page(t, c):
             nc.scalar.activation(
-                z_pairs[c][:, t // 2, :, t % 2],
+                z_pairs[c].bitcast(BF16).rearrange("p (u w e) -> p u w e", u=2, e=2)[:, t // 2, :, t % 2],
                 pages[t][:, c * SLOT_CHUNK : (c + 1) * SLOT_CHUNK],
                 ACT.Copy,
                 scale=ga_signed[:, t : t + 1],
@@ -165,7 +161,7 @@ def tile_picked_keypage_none_p_kernel(
             grouped = sb(f"z_grouped{c}", [P, SLOT_CHUNK * PACK], BF16)
             nc.scalar.copy(
                 grouped[:].bitcast(F32).rearrange("p (c i u) -> p c u i", i=4, u=2),
-                z_pairs[c][:].rearrange("p u w e -> p u (w e)").bitcast(F32).rearrange("p u (c i) -> p c u i", i=4),
+                z_pairs[c].rearrange("p (u c i) -> p c u i", u=2, i=4),
             )
             return grouped
 
@@ -175,9 +171,12 @@ def tile_picked_keypage_none_p_kernel(
         nc.scalar.copy(dst, src)
         write_page(1)
         w2_q = quantize("w2", w2_grouped[:], H)
-        z_pairs.append(sb("z_pairs0", [P, 2, SLOT_CHUNK, 2], BF16, reuse="w2_raw"))
-        z_pairs.append(sb("z_pairs1", [P, 2, SLOT_CHUNK, 2], BF16, reuse="w2_grouped"))
+        early = 2 * QUERY_CHUNKS[1]
+        late = sb("late", [P, early + 4 * SLOT_CHUNK], F32, reuse="w2_raw")
+        z_pairs.append(late[:, early + 2 * SLOT_CHUNK :])
+        z_pairs.append(late[:, early : early + 2 * SLOT_CHUNK])
         scale_page(0, 0)
+        scale_page(0, 1)
         b_rows = []
         b_all = sb("b_all", [P, PACK, V], F32)
         for t in range(PACK):
@@ -187,7 +186,6 @@ def tile_picked_keypage_none_p_kernel(
             nc.scalar.activation(b_t[:], acc[:], ACT.Copy, scale=gb_abs[:, t : t + 1])
             nc.sync.dma_start(b_all[:, t, :], b_t[:])
             b_rows.append(b_t)
-        scale_page(0, 1)
         for t in range(1, PACK):
             if t > 1:
                 write_page(t)
@@ -196,41 +194,56 @@ def tile_picked_keypage_none_p_kernel(
                 if t == PACK - 1:
                     z_grouped.append(group_page(c))
 
-        def neighbours(n, v0, width):
-            reuse = ("a3", "z_grouped1", None)[n]
-            fetched = sb(f"fetched{n}", [P, PACK, width], F32, reuse=reuse)
+        def fetch_neighbours(n, order):
+            v0, width = sum(QUERY_CHUNKS[:n]), QUERY_CHUNKS[n]
+            room = a_all[:, 2 * S :] if n == 0 else late[:, (n - 1) * width : (n - 1 + PACK) * width]
+            fetched = room.rearrange("p (t v) -> p t v", t=PACK)
             columns = slice(v0 // PER_COLUMN, (v0 + width) // PER_COLUMN)
-            for t in range(PACK):
+            for t in order:
                 nc.vector.tensor_copy(fetched[:, t, :], b_rows[t][:].indirect(nq_list[:, columns]))
+            return fetched
+
+        def larger(n, fetched):
+            v0, width = sum(QUERY_CHUNKS[:n]), QUERY_CHUNKS[n]
             grouped = sb(f"z2_grouped{n}", [P, width * PACK], BF16)
             nc.vector.tensor_tensor(
                 grouped[:].rearrange("p (c i t) -> p c t i", i=4, t=PACK),
                 b_all[:, :, v0 : v0 + width].rearrange("p t (c i) -> p c t i", i=4),
-                fetched[:].rearrange("p t (c i) -> p c t i", i=4),
+                fetched.rearrange("p t (c i) -> p c t i", i=4),
                 ALU.max,
             )
-            return grouped
+            return quantize(f"z2_{n}", grouped[:], width)
 
         out_rows = out.rearrange("(b p) v -> p b v", p=P)
         blocks_per_chunk = SLOT_CHUNK // P
-        z_q = []
-        next_bank = 0
-        v0 = 0
-        for n, width in enumerate(QUERY_CHUNKS):
-            z2_grouped = neighbours(n, v0, width)
-            if n == 0:
-                z_q.append(quantize("z0", z_grouped[0][:], SLOT_CHUNK))
-            z2_q = quantize(f"z2_{n}", z2_grouped[:], width)
-            if n == 0:
-                z_q.append(quantize("z1", z_grouped[1][:], SLOT_CHUNK))
-            per_bank = BANK // width
-            for first in range(0, U // P, per_bank):
-                acc = bank(next_bank)
+        used_banks = []
+
+        def score(z_q, c, z2_q, n, per_bank):
+            v0, width = sum(QUERY_CHUNKS[:n]), QUERY_CHUNKS[n]
+            for first in range(0, blocks_per_chunk, per_bank):
+                acc = bank(len(used_banks) % 8)
                 for g in range(per_bank):
-                    c, block = divmod(first + g, blocks_per_chunk)
-                    product(acc[:, g * width : (g + 1) * width], z_q[c], slice(P * block, P * (block + 1)), z2_q)
-                scores = sb(f"scores{next_bank}", [P, per_bank, width], F32)
-                nc.scalar.activation(scores[:].rearrange("p g v -> p (g v)"), acc[:], ACT.Tanh, scale=0.0625)
-                nc.sync.dma_start(out_rows[:, first : first + per_bank, v0 : v0 + width], scores[:])
-                next_bank = next_bank + 1
-            v0 = v0 + width
+                    block = first + g
+                    product(acc[:, g * width : (g + 1) * width], z_q, slice(P * block, P * (block + 1)), z2_q)
+                scores = sb(f"scores{len(used_banks)}", [P, per_bank, width], F32)
+                nc.scalar.activation(
+                    scores[:].rearrange("p g v -> p (g v)"), acc[:, : per_bank * width], ACT.Tanh, scale=0.0625
+                )
+                row = c * blocks_per_chunk + first
+                nc.sync.dma_start(out_rows[:, row : row + per_bank, v0 : v0 + width], scores[:])
+                used_banks.append(acc)
+
+        fetched = fetch_neighbours(0, range(PACK))
+        z2_first = larger(0, fetched)
+        z_q = [quantize("z0", z_grouped[0][:], SLOT_CHUNK)]
+        score(z_q[0], 0, z2_first, 0, 2)
+        fetched = fetch_neighbours(1, range(PACK))
+        z_q.append(quantize("z1", z_grouped[1][:], SLOT_CHUNK))
+        score(z_q[1], 1, z2_first, 0, 2)
+        z2_second = larger(1, fetched)
+        for c in range(slot_chunks):
+            score(z_q[c], c, z2_second, 1, 4)
+        fetched = fetch_neighbours(2, (3, 0, 1, 2))
+        z2_third = larger(2, fetched)
+        for c in range(slot_chunks):
+            score(z_q[c], c, z2_third, 2, 2)

@@ -19,7 +19,7 @@ BANK = 512
 PER_COLUMN = 16
 FLOPS = 2 * K * H * S + 2 * K * H * V + 2 * H * U * V
 
-W1_VECTOR_M = 24
+W1_VECTOR_M = 40
 SLOT_CHUNK = 512
 QUERY_CHUNKS = (256, 128, 128)
 
@@ -65,13 +65,13 @@ def tile_picked_keypage_none_p_kernel(
             nc.vector.quantize_mx(out=codes[:].bitcast(FP8X4), scales=scales[:], in_=grouped)
             return codes, scales
 
-        def product(acc, stationary, columns, moving):
+        def product(acc, stationary, columns, moving, moving_columns=slice(None)):
             nc.tensor.matmul_mx(
                 out=acc,
                 lhsT=stationary[0][:, columns].bitcast(FP8X4),
                 lhsT_scale=stationary[1][:, columns],
-                rhs=moving[0][:].bitcast(FP8X4),
-                rhs_scale=moving[1][:],
+                rhs=moving[0][:, moving_columns].bitcast(FP8X4),
+                rhs_scale=moving[1][:, moving_columns],
                 start=True,
                 stop=True,
             )
@@ -119,17 +119,28 @@ def tile_picked_keypage_none_p_kernel(
                 raw[:].rearrange("p j (m t) -> p m j t", t=PACK),
             )
 
-        w1_grouped = sb("w1_grouped", [P, PACK * H], BF16)
-        dst, src = cast_views(w1_raw, w1_grouped)
-        nc.vector.tensor_copy(dst[:, :W1_VECTOR_M], src[:, :W1_VECTOR_M])
-        nc.scalar.copy(dst[:, W1_VECTOR_M:], src[:, W1_VECTOR_M:])
+        w1_grouped = [sb(f"w1_grouped{u}", [P, PACK * H // 2], BF16) for u in range(2)]
+        src = w1_raw[:].rearrange("p j (m t) -> p m j t", t=PACK)
+        dst = [half[:].rearrange("p (t m j) -> p m j t", t=2, j=PACK) for half in w1_grouped]
+        nc.vector.tensor_copy(dst[0][:, :W1_VECTOR_M], src[:, :W1_VECTOR_M, :, :2])
+        nc.scalar.copy(dst[0][:, W1_VECTOR_M:], src[:, W1_VECTOR_M:, :, :2])
+        nc.scalar.copy(dst[1], src[:, :, :, 2:])
 
-        xa = (gather("xa_words", x_word_table, offs_list, U32), xa_scales)
-        half = PACK * H // 2
-        w1_q = [quantize(f"w1_{u}", w1_grouped[:, u * half : (u + 1) * half], H // 2) for u in range(2)]
+        w1_q = [quantize("w1_0", w1_grouped[0][:], H // 2)]
+        xa_words = sb("xa_words", [P, S], U32)
+        halves = [slice(h * S // 2, (h + 1) * S // 2) for h in range(2)]
+        for h in halves:
+            offsets = offs_list[:, h.start // PER_COLUMN : h.stop // PER_COLUMN]
+            nc.vector.tensor_copy(xa_words[:, h], x_word_table[:].indirect(offsets))
+        w1_q.append(quantize("w1_1", w1_grouped[1][:], H // 2))
+        xa = (xa_words, xa_scales)
         a_all = sb("a_all", [P, PACK * S], F32)
         a_rows = [a_all[:, S * t : S * (t + 1)] for t in range(PACK)]
-        for t in range(PACK):
+        for i, h in enumerate(halves):
+            acc = bank(PACK * i)
+            product(acc[:, h], w1_q[0], slice(0, P), xa, h)
+            nc.scalar.copy(a_all[:, h], acc[:, h])
+        for t in range(1, PACK):
             acc = bank(t)
             product(acc[:], w1_q[t // 2], slice(P * (t % 2), P * (t % 2 + 1)), xa)
             nc.scalar.copy(a_rows[t], acc[:])

from contextlib import ExitStack

import concourse.mybir as mybir

F32 = mybir.dt.float32
BF16 = mybir.dt.bfloat16
I32 = mybir.dt.int32
U32 = mybir.dt.uint32
U16 = mybir.dt.uint16
U8 = mybir.dt.uint8
FP8X4 = mybir.dt.float8_e4m3fn_x4
ALU = mybir.AluOpType
ACT = mybir.ActivationFunctionType

K, T, S, V, H, U = 512, 2048, 512, 512, 512, 1024
P = 128
PACK = 4
BANK = 512
PER_COLUMN = 16
FLOPS = 2 * K * H * S + 2 * K * H * V + 2 * H * U * V

W1_VECTOR_M = 40
SLOT_CHUNK = 512
QUERY_CHUNKS = (256, 128, 128)


def tile_picked_keypage_none_p_kernel(
    tc, x_words, x_scales, w1, w2, mem, ga, gb, offs, two, slot, nq, out
):
    nc = tc.nc
    with ExitStack() as ctx:
        lists = ctx.enter_context(tc.tile_pool(name="lists", bufs=1))
        keep = ctx.enter_context(tc.tile_pool(name="keep", bufs=1))
        psum = ctx.enter_context(tc.psum_pool(name="psum", bufs=1))

        def sb(name, shape, dtype, reuse=None):
            return keep.tile(shape, dtype, name=name, tag=reuse or name, align_bytes=64)

        def bank(i):
            return psum.tile([P, BANK], F32, name=f"bank{i}", tag=f"bank{i}")

        def load_list(name, source):
            tile = lists.tile([P, S // PER_COLUMN], U16, name=name)
            nc.sync.dma_start(tile[:], source)
            return tile

        def load_weight(name, w):
            raw = sb(name, [P, PACK, H], F32)
            nc.sync.dma_start(raw[:], w.rearrange("(p j) c -> p j c", j=PACK))
            return raw

        def load_feature_weights(name, g):
            tile = sb(name, [P, PACK], F32)
            nc.sync.dma_start(tile[:], g.rearrange("(p t) o -> p (t o)", t=PACK))
            return tile

        def load_page(t):
            tile = sb(f"page{t}", [P, U], F32)
            nc.sync.dma_start(tile[:], mem.rearrange("(p t) w -> p t w", t=PACK)[:, t, :])
            return tile

        def quantize(name, grouped, width):
            codes = sb(f"{name}_codes", [P, width], U32)
            scales = sb(f"{name}_scales", [P, width], U8)
            nc.vector.quantize_mx(out=codes[:].bitcast(FP8X4), scales=scales[:], in_=grouped)
            return codes, scales

        def product(acc, stationary, columns, moving, moving_columns=slice(None)):
            nc.tensor.matmul_mx(
                out=acc,
                lhsT=stationary[0][:, columns].bitcast(FP8X4),
                lhsT_scale=stationary[1][:, columns],
                rhs=moving[0][:, moving_columns].bitcast(FP8X4),
                rhs_scale=moving[1][:, moving_columns],
                start=True,
                stop=True,
            )

        x_word_table = sb("x_word_table", [P, T], U32)
        x_word_rows = x_words[0].rearrange("p n r -> p (n r)").bitcast(I32)
        nc.sync.dma_start(x_word_table[:, : T // 2].bitcast(I32), x_word_rows[:, : T // 2])
        offs_list = load_list("offs_list", offs)
        two_list = load_list("two_list", two)
        x_scale_table = sb("x_scale_table", [P, T], U8)
        nc.vector.memset(x_scale_table[:].bitcast(I32), 0)
        for q in range(4):
            nc.sync.dma_start(
                x_scale_table[32 * q : 32 * q + 4, :].bitcast(I32),
                x_scales[0, 4 * q : 4 * q + 4, :].bitcast(I32),
            )
        warm = sb("warm", [P, 1], F32)
        warm_out = sb("warm_out", [P, 1], F32)
        nc.gpsimd.memset(warm[:], 0.0)
        nc.scalar.activation(warm_out[:], warm[:], ACT.Tanh)

        w1_raw = load_weight("w1_raw", w1)
        nc.sync.dma_start(x_word_table[:, T // 2 :].bitcast(I32), x_word_rows[:, T // 2 :])
        ga_raw = load_feature_weights("ga_raw", ga)
        gb_raw = load_feature_weights("gb_raw", gb)
        slot_list = load_list("slot_list", slot)
        pages = [load_page(0)]
        w2_raw = load_weight("w2_raw", w2)
        pages.append(load_page(1))
        pages.append(load_page(2))
        pages.append(load_page(3))
        nq_list = load_list("nq_list", nq)

        def gather(name, table, offsets, dtype, reuse=None):
            picked = sb(name, [P, S], dtype, reuse=reuse)
            nc.vector.tensor_copy(picked[:], table[:].indirect(offsets[:]))
            return picked

        xa_scales = gather("xa_scales", x_scale_table, offs_list, U8)
        xb_scales = gather("xb_scales", x_scale_table, two_list, U8)

        def cast_views(raw, grouped):
            return (
                grouped[:].rearrange("p (t m j) -> p m j t", t=PACK, j=PACK),
                raw[:].rearrange("p j (m t) -> p m j t", t=PACK),
            )

        w1_grouped = [sb(f"w1_grouped{u}", [P, PACK * H // 2], BF16) for u in range(2)]
        src = w1_raw[:].rearrange("p j (m t) -> p m j t", t=PACK)
        dst = [half[:].rearrange("p (t m j) -> p m j t", t=2, j=PACK) for half in w1_grouped]
        nc.vector.tensor_copy(dst[0][:, :W1_VECTOR_M], src[:, :W1_VECTOR_M, :, :2])
        nc.scalar.copy(dst[0][:, W1_VECTOR_M:], src[:, W1_VECTOR_M:, :, :2])
        nc.scalar.copy(dst[1], src[:, :, :, 2:])

        w1_q = [quantize("w1_0", w1_grouped[0][:], H // 2)]
        xa_words = sb("xa_words", [P, S], U32)
        halves = [slice(h * S // 2, (h + 1) * S // 2) for h in range(2)]
        for h in halves:
            offsets = offs_list[:, h.start // PER_COLUMN : h.stop // PER_COLUMN]
            nc.vector.tensor_copy(xa_words[:, h], x_word_table[:].indirect(offsets))
        w1_q.append(quantize("w1_1", w1_grouped[1][:], H // 2))
        xa = (xa_words, xa_scales)
        a_all = sb("a_all", [P, PACK * S], F32)
        a_rows = [a_all[:, S * t : S * (t + 1)] for t in range(PACK)]
        for i, h in enumerate(halves):
            acc = bank(PACK * i)
            product(acc[:, h], w1_q[0], slice(0, P), xa, h)
            nc.scalar.copy(a_all[:, h], acc[:, h])
        for t in range(1, PACK):
            acc = bank(t)
            product(acc[:], w1_q[t // 2], slice(P * (t % 2), P * (t % 2 + 1)), xa)
            nc.scalar.copy(a_rows[t], acc[:])
        xb = (gather("xb_words", x_word_table, two_list, U32, reuse="w1_raw"), xb_scales)

        twice_nonneg = sb("twice_nonneg", [P, PACK], F32)
        ga_signed = sb("ga_signed", [P, PACK], F32)
        gb_abs = sb("gb_abs", [P, PACK], F32)
        nc.vector.tensor_scalar(twice_nonneg[:], gb_raw[:], 0.0, 2.0, ALU.is_ge, ALU.mult)
        nc.vector.scalar_tensor_tensor(ga_signed[:], twice_nonneg[:], -1.0, ga_raw[:], ALU.add, ALU.mult)
        nc.vector.scalar_tensor_tensor(gb_abs[:], twice_nonneg[:], -1.0, gb_raw[:], ALU.add, ALU.mult)

        slot_chunks = U // SLOT_CHUNK
        z_pairs = []
        z_grouped = []

        def write_page(t):
            nc.vector.tensor_copy(pages[t][:].indirect(slot_list[:]), a_rows[t])

        def scale_page(t, c):
            nc.scalar.activation(
                z_pairs[c].bitcast(BF16).rearrange("p (u w e) -> p u w e", u=2, e=2)[:, t // 2, :, t % 2],
                pages[t][:, c * SLOT_CHUNK : (c + 1) * SLOT_CHUNK],
                ACT.Copy,
                scale=ga_signed[:, t : t + 1],
            )

        def group_page(c):
            grouped = sb(f"z_grouped{c}", [P, SLOT_CHUNK * PACK], BF16)
            nc.scalar.copy(
                grouped[:].bitcast(F32).rearrange("p (c i u) -> p c u i", i=4, u=2),
                z_pairs[c].rearrange("p (u c i) -> p c u i", u=2, i=4),
            )
            return grouped

        write_page(0)
        w2_grouped = sb("w2_grouped", [P, PACK * H], BF16)
        dst, src = cast_views(w2_raw, w2_grouped)
        nc.scalar.copy(dst, src)
        write_page(1)
        w2_q = quantize("w2", w2_grouped[:], H)
        early = 2 * QUERY_CHUNKS[1]
        late = sb("late", [P, early + 4 * SLOT_CHUNK], F32, reuse="w2_raw")
        z_pairs.append(late[:, early + 2 * SLOT_CHUNK :])
        z_pairs.append(late[:, early : early + 2 * SLOT_CHUNK])
        scale_page(0, 0)
        scale_page(0, 1)
        b_rows = []
        b_all = sb("b_all", [P, PACK, V], F32)
        for t in range(PACK):
            acc = bank(PACK + t)
            product(acc[:], w2_q, slice(P * t, P * (t + 1)), xb)
            b_t = sb(f"b{t}", [P, V], F32)
            nc.scalar.activation(b_t[:], acc[:], ACT.Copy, scale=gb_abs[:, t : t + 1])
            nc.sync.dma_start(b_all[:, t, :], b_t[:])
            b_rows.append(b_t)
        for t in range(1, PACK):
            if t > 1:
                write_page(t)
            for c in range(slot_chunks):
                scale_page(t, c)
                if t == PACK - 1:
                    z_grouped.append(group_page(c))

        def fetch_neighbours(n, order):
            v0, width = sum(QUERY_CHUNKS[:n]), QUERY_CHUNKS[n]
            room = a_all[:, 2 * S :] if n == 0 else late[:, (n - 1) * width : (n - 1 + PACK) * width]
            fetched = room.rearrange("p (t v) -> p t v", t=PACK)
            columns = slice(v0 // PER_COLUMN, (v0 + width) // PER_COLUMN)
            for t in order:
                nc.vector.tensor_copy(fetched[:, t, :], b_rows[t][:].indirect(nq_list[:, columns]))
            return fetched

        def larger(n, fetched):
            v0, width = sum(QUERY_CHUNKS[:n]), QUERY_CHUNKS[n]
            grouped = sb(f"z2_grouped{n}", [P, width * PACK], BF16)
            nc.vector.tensor_tensor(
                grouped[:].rearrange("p (c i t) -> p c t i", i=4, t=PACK),
                b_all[:, :, v0 : v0 + width].rearrange("p t (c i) -> p c t i", i=4),
                fetched.rearrange("p t (c i) -> p c t i", i=4),
                ALU.max,
            )
            return quantize(f"z2_{n}", grouped[:], width)

        out_rows = out.rearrange("(b p) v -> p b v", p=P)
        blocks_per_chunk = SLOT_CHUNK // P
        used_banks = []

        def score(z_q, c, z2_q, n, per_bank):
            v0, width = sum(QUERY_CHUNKS[:n]), QUERY_CHUNKS[n]
            for first in range(0, blocks_per_chunk, per_bank):
                acc = bank(len(used_banks) % 8)
                for g in range(per_bank):
                    block = first + g
                    product(acc[:, g * width : (g + 1) * width], z_q, slice(P * block, P * (block + 1)), z2_q)
                scores = sb(f"scores{len(used_banks)}", [P, per_bank, width], F32)
                nc.scalar.activation(
                    scores[:].rearrange("p g v -> p (g v)"), acc[:, : per_bank * width], ACT.Tanh, scale=0.0625
                )
                row = c * blocks_per_chunk + first
                nc.sync.dma_start(out_rows[:, row : row + per_bank, v0 : v0 + width], scores[:])
                used_banks.append(acc)

        fetched = fetch_neighbours(0, range(PACK))
        z2_first = larger(0, fetched)
        z_q = [quantize("z0", z_grouped[0][:], SLOT_CHUNK)]
        score(z_q[0], 0, z2_first, 0, 2)
        fetched = fetch_neighbours(1, range(PACK))
        z_q.append(quantize("z1", z_grouped[1][:], SLOT_CHUNK))
        score(z_q[1], 1, z2_first, 0, 2)
        z2_second = larger(1, fetched)
        for c in range(slot_chunks):
            score(z_q[c], c, z2_second, 1, 4)
        fetched = fetch_neighbours(2, (3, 0, 1, 2))
        z2_third = larger(2, fetched)
        for c in range(slot_chunks):
            score(z_q[c], c, z2_third, 2, 2)
